import numpy as np, ml_dtypes
CORES = [3,7,11,15,131,135,139,143]
N = 8
import mx_ref
BF = ml_dtypes.bfloat16
def entries(a):
    return np.ascontiguousarray(a.T).reshape(-1)
def table(e):
    return np.ascontiguousarray(np.reshape(e, (-1, 16)).T).astype(np.int32)
def cols(t, e):
    v = np.concatenate([t.reshape(128, -1, 4), np.zeros((128, 1, 4), BF)], axis=1)
    return np.ascontiguousarray(v[:, e]).reshape(128, -1)
def f(rng, *shape):
    return mx_ref.flush((rng.standard_normal(shape, dtype=np.float32) * np.exp2(rng.integers(-2, 3, shape[:-1] + (1,)))).astype(BF))
def wide(rng, *shape, cols=0):
    v = rng.standard_normal(shape, dtype=np.float32) * np.exp2(rng.integers(-12, 13, shape)).astype(np.float32)
    if cols: v *= np.repeat(np.exp2(rng.integers(-cols, cols + 1, shape[:-2] + (1, shape[-1] // 4))) * (rng.random(shape[:-2] + (1, shape[-1] // 4)) > 0.0625), 4, axis=-1).astype(np.float32)
    return mx_ref.flush(v.astype(BF))
T, S, CAPP = 512, 256, 48
def lists(rng, most=None, own=False, share=False, edge=False):
    o, c, m = [], [], []
    for r in range(N):
        n = np.zeros(N, int)
        if own: n[r] = CAPP
        if most is not None:
            for q in rng.permutation(N)[:most]: n[q] = CAPP
            n = np.minimum(n, np.maximum(0, S - (np.cumsum(n) - n)))
        while n.sum() < S:
            q = rng.integers(0, N)
            if n[q] < CAPP: n[q] += 1
        slots = np.full(N * CAPP, -1); used = []
        for q in range(N):
            k = q * CAPP + rng.permutation(CAPP)[:n[q]]; used += list(k)
            slots[k] = rng.integers(0, T) if share else rng.choice([0, T - 1], n[q]) if edge else rng.integers(0, T, n[q])
        o.append(table(rng.choice([0, T - 1], S) if edge else rng.integers(0, T, S))); c.append(table(slots)); m.append(table(rng.permutation(used)))
    return {"own": np.stack(o), "want": np.stack(c), "slot": np.stack(m)}
def setup_inputs(rng):
    return {"x": f(rng, N, 128, 4 * T), "w": f(rng, N, 128, 512), **lists(rng)}
def setup_inputs_edge(rng):
    return {**setup_inputs(rng), **lists(rng, edge=True)}
def setup_inputs_full(rng):
    return {**setup_inputs(rng), **lists(rng, most=S // CAPP)}
def setup_inputs_self(rng):
    return {**setup_inputs(rng), **lists(rng, own=True)}
def setup_inputs_share(rng):
    return {**setup_inputs(rng), **lists(rng, share=True)}
def setup_inputs_spread(rng):
    d = setup_inputs(rng); d["x"] = wide(rng, N, 128, 4 * T, cols=8); return d
def check_inputs(d):
    b = []
    for r in range(N):
        o, c, m = entries(d["own"][r]), entries(d["want"][r]), entries(d["slot"][r])
        if o.min() < 0 or o.max() >= T: b.append("own")
        if c.min() < -1 or c.max() >= T: b.append("want")
        if m.min() < 0 or m.max() >= N * CAPP or len(set(m.tolist())) != S or (c[m] < 0).any() or (c >= 0).sum() != S: b.append("slot")
    return b
def decode(q):
    out = np.zeros(q[0].shape, np.float32)
    for b in range(4):
        e = np.zeros((128, 128, 4), np.float32); e[np.arange(128), np.arange(128), b] = 1
        out[:, b::4] = mx_ref.matmul(mx_ref.quantize(e.reshape(128, 512).astype(BF)), q)
    return out
def reference(x, w, own, want, slot):
    M = []
    for r in range(N):
        c = entries(want[r])
        arrived = np.concatenate([decode(mx_ref.quantize(cols(x[q], c[q * CAPP:(q + 1) * CAPP]))) for q in range(N)], axis=1)
        far = arrived.reshape(128, -1, 4)[:, entries(slot[r])].reshape(128, -1)
        M.append(mx_ref.quantize(((cols(x[r], entries(own[r])).astype(np.float32) + far) * np.float32(0.5)).astype(BF)))
    y = np.zeros((N, 128, 3 * S), np.float32)
    for r in range(N):
        for i in range(3): y[r][:, S * i:S * i + S] = mx_ref.matmul(mx_ref.quantize(w[r]), M[(r - 1 + i) % N])
    return {"y": y}

from concourse.bass import DstId, RemoteDMATransfer, IndirectOffsetOnAxis
from concourse.mybir import dt, AluOpType, ActivationFunctionType

N, CAPP, S, XC = 8, 48, 256, 512
G = 4
H = S // 2

SCRATCH = {
    "wl": ("sbuf", [128, 24], "int32"),
    "ol": ("sbuf", [128, 16], "int32"),
    "sl": ("sbuf", [128, 16], "int32"),
    "lf": ("sbuf", [128, 12], "int32"),
    "ln": ("sbuf", [128, 12], "int32"),
    "fo": ("sbuf", [128, 12], "uint16"),
    "no": ("sbuf", [128, 16], "uint16"),
    "wo": ("sbuf", [128, 8], "uint16"),
    "oo": ("sbuf", [128, 16], "uint16"),
    "so": ("sbuf", [128, 16], "uint16"),
    "xt": ("sbuf", [128, 4 * XC], "bfloat16"),
    "wt": ("sbuf", [128, 512], "bfloat16"),
    "wq": ("sbuf", [128, 128], "float8_e4m3fn_x4"),
    "ws": ("sbuf", [128, 128], "uint8"),
    "e1": ("sbuf", [128, 520], "bfloat16"),
    "e2": ("sbuf", [128, 520], "bfloat16"),
    "eq": ("sbuf", [128, 512], "float8_e4m3fn_x4"),
    "es": ("sbuf", [128, 512], "uint8"),
    "hf": ("sbuf", [128, 4 * 192], "bfloat16"),
    "hn": ("sbuf", [128, 4 * 144], "bfloat16"),
    "ho": ("sbuf", [128, 512], "bfloat16"),
    "qf": ("sbuf", [128, 192], "float8_e4m3fn_x4"),
    "qfs": ("sbuf", [128, 192], "uint8"),
    "qn": ("sbuf", [128, 144], "float8_e4m3fn_x4"),
    "qns": ("sbuf", [128, 144], "uint8"),
    "qo": ("sbuf", [128, 128], "float8_e4m3fn_x4"),
    "qos": ("sbuf", [128, 128], "uint8"),
    "cf": ("sbuf", [128, 192], "float8_e4m3fn_x4"),
    "cfs": ("sbuf", [128, 192], "uint8"),
    "cn": ("sbuf", [128, 192], "float8_e4m3fn_x4"),
    "cns": ("sbuf", [128, 192], "uint8"),
    "dw": ("sbuf", [128, 4 * N * CAPP], "float32"),
    "xo": ("sbuf", [128, 4 * S], "float32"),
    "m": ("sbuf", [128, 4 * S], "bfloat16"),
    "mq": ("sbuf", [128, S], "float8_e4m3fn_x4"),
    "ms": ("sbuf", [128, S], "uint8"),
    "iq": ("sbuf", [128, S], "float8_e4m3fn_x4"),
    "is_": ("sbuf", [128, S], "uint8"),
    "oq": ("sbuf", [128, S], "float8_e4m3fn_x4"),
    "os_": ("sbuf", [128, S], "uint8"),
    "yo": ("sbuf", [128, S], "float32"),
    "yi": ("sbuf", [128, S], "float32"),
    "yf": ("sbuf", [128, S], "float32"),
    "pf": ("psum", [128, 2048], "float32"),
    "pn": ("psum", [128, 2048], "float32"),
}
SEMAPHORES = (["want", "xl", "own", "slot", "wl", "sent", "lf", "ln", "cf", "cn", "mi", "mo", "e1", "e2", "eq", "wq",
               "hoz", "cvw", "cvo", "cvs", "cvf", "cvn", "gfv", "gfs", "gnv", "gns", "gos", "qf", "qn", "qo", "oc", "q0", "q1",
               "yo", "yi", "yf0", "yf1", "po", "pi", "pf0", "pf1", "st1", "st2"]
              + ["df%d" % b for b in range(4)] + ["dn%d" % b for b in range(4)]
              + ["wf%d" % b for b in range(4)] + ["wn%d" % b for b in range(4)]
              + ["xo%d" % b for b in range(4)] + ["ga0", "ga1"])


def bits(engines):
    m = 0
    for e in engines:
        m |= 1 << e
    return m


def rank_program(g, core, T, topo):
    r = T.rank_of(core)
    if r is None:
        return
    sem = T.sem
    v, a, pe, sy = g.vector, g.scalar, g.tensor, g.sync
    COPY = ActivationFunctionType.Copy
    cores = T.cores

    host = [q for q in range(N) if topo.host(cores[q]) == topo.host(core)]
    far = [q for q in range(N) if q not in host]
    near = [q for q in host if q != r]
    mates = [q for q in near if topo.mates(core, cores[q])]
    partner = [q for q in near if q not in mates][0]
    left, right = (r - 1) % N, (r + 1) % N
    away = left if right == partner else right
    off_eng = topo.engines(core, cores[far[0]])
    on_eng = [e for e in topo.engines(core, cores[partner]) if e not in off_eng]
    me = host.index(r)

    def near_index(q, s):
        return [t for t in range(N) if topo.host(cores[t]) == topo.host(cores[q]) and t != q].index(s)

    def dst(q):
        rid, pid = topo.addr(cores[q], core)
        return [DstId(rid=rid, pnc=pid)]

    sent = [0]

    def fused(parts):
        ts = []
        for q, eng, s, src, d in parts:
            ts.append(RemoteDMATransfer(dst_ids=dst(q), dma_engine_mask=bits(eng), remote_sem=s, src=src, dst=d))
            sent[0] += len(eng)
        g.remote_dma_fused(ts, local_sem=sem.sent)

    def u8(x):
        return x.bitcast(dt.uint8)

    two = len(off_eng) // len(far)
    four = len(off_eng) // len(mates)
    feng = {q: off_eng[two * i:two * i + two] for i, q in enumerate(far)}
    neng = {q: off_eng[four * i:four * i + four] for i, q in enumerate(mates)}
    neng[partner] = on_eng

    for k in range(4):
        sy.dma_start(T.wl[16 * k:16 * k + 16, :], T.want[:]).then_inc(sem.want, 16)
    for k in range(4, 8):
        a.dma_start(T.wl[16 * k:16 * k + 16, :], T.want[:]).then_inc(sem.want, 16)
    sy.dma_start(T.xt[:], T.x[:]).then_inc(sem.xl, 16)
    for k in range(8):
        sy.dma_start(T.ol[16 * k:16 * k + 16, :], T.own[:]).then_inc(sem.own, 16)
    for k in range(8):
        sy.dma_start(T.sl[16 * k:16 * k + 16, :], T.slot[:]).then_inc(sem.slot, 16)
    sy.dma_start(T.wt[:], T.w[:]).then_inc(sem.wl, 16)

    g.wait_ge(sem.want, 128)

    def wslice(q):
        return T.wl[:, 3 * q:3 * q + 3]

    fused([(q, feng[q], sem.lf, wslice(q), T.lf[:, 3 * me:3 * me + 3]) for q in far])

    def nlist(q):
        k = near_index(q, r)
        return (q, neng[q], sem.ln, wslice(q), T.ln[:, 3 * k:3 * k + 3])

    fused([nlist(q) for q in mates])
    fused([nlist(partner)])
    g.wait_ge(sem.e1, 1)
    g.affine_select(T.e2[:], T.e1[:], [[-1, 520]], AluOpType.is_equal, 0.0, 3, 4).then_inc(sem.e2, 1)

    g.wait_ge(sem.qf, 1)

    def cols(q, eng, buf, i, land, s):
        c, d = CAPP * i, CAPP * me
        return [(q, eng, s, u8(T[buf][:, c:c + CAPP]), u8(T[land][:, d:d + CAPP])),
                (q, eng, s, T[buf + "s"][:, c:c + CAPP], T[land + "s"][:, d:d + CAPP])]

    fc = [cols(q, feng[q], "qf", i, "cf", sem.cf) for i, q in enumerate(far)]
    fused([p[0] for p in fc])
    fused([p[1] for p in fc])
    g.wait_ge(sem.qn, 1)
    nc = [cols(q, neng[q], "qn", i, "cn", sem.cn) for i, q in enumerate(near)]
    fused([p[0] for p in nc])
    fused([p[1] for p in nc])

    def mout(lo, hi, scales):
        if scales:
            s, i, o = T.ms[:, lo:hi], T.is_[:, lo:hi], T.os_[:, lo:hi]
        else:
            s, i, o = u8(T.mq[:, lo:hi]), u8(T.iq[:, lo:hi]), u8(T.oq[:, lo:hi])
        fused([(away, off_eng, sem.mo, s, o), (partner, on_eng, sem.mi, s, i)])

    g.wait_ge(sem.q0, 1)
    mout(0, H, False)
    g.wait_ge(sem.q1, 1)
    mout(H, S, False)
    mout(0, S, True)
    g.wait_ge(sem.sent, sent[0])

    def sgather(out, off, t, scale=None):
        w = T.xt[:, t:4 * XC].indirect(off)
        if scale is None:
            return a.activation(out, w, COPY)
        return a.activation(out, w, COPY, scale=scale)

    a.wait_ge(sem.xl, 16)
    a.wait_ge(sem.cvf, 1)
    for t in (2, 3):
        sgather(T.hf[:, t:768:4], T.fo[:, 0:12], t).then_inc(sem.gfs, 1)
    a.wait_ge(sem.cvn, 1)
    for t in (2, 3):
        sgather(T.hn[:, t:576:4], T.no[:, 0:9], t).then_inc(sem.gns, 1)
    a.wait_ge(sem.hoz, 1)
    a.wait_ge(sem.cvw, 1)
    for t in range(4):
        sgather(T.ho[:, t:192:4], T.wo[:, 0:3], t).then_inc(sem.gos, 1)
    a.wait_ge(sem.cvo, 1)
    for t in range(4):
        sgather(T.xo[:, S * t:S * t + S], T.oo[:, 0:16], t, 0.5).then_inc(sem["xo%d" % t], 1)

    def window(b, grp):
        base = N * CAPP * b + CAPP * grp[0]
        return T.dw[:, base:base + CAPP * G]

    for b in (0, 2):
        a.wait_ge(sem["df%d" % b], 1)
        a.activation(window(b, far), T.pf[:, 512 * b:512 * b + 192], COPY).then_inc(sem["wf%d" % b], 1)
    for b in range(4):
        a.wait_ge(sem["dn%d" % b], 1)
        a.activation(window(b, host), T.pn[:, 512 * b:512 * b + 192], COPY).then_inc(sem["wn%d" % b], 1)
    a.wait_ge(sem.po, 1)
    a.activation(T.yo[:], T.pf[:, 0:S], COPY).then_inc(sem.yo, 1)
    a.wait_ge(sem.pf1, 1)
    a.activation(T.yf[:, H:S], T.pf[:, 1536:1536 + H], COPY).then_inc(sem.yf1, 1)
    slot_i, slot_o = (0, 2) if partner == left else (2, 0)
    a.wait_ge(sem.yf1, 1)
    a.dma_start(T.y[:, S * slot_o + H:S * slot_o + S], T.yf[:, H:S]).then_inc(sem.st2, 16)
    a.wait_ge(sem.st2, 16)

    sy.wait_ge(sem.qo, 1)
    sy.dma_start(u8(T.cn[:, CAPP * me:CAPP * me + CAPP]), u8(T.qo[:, 0:CAPP])).then_inc(sem.oc, 16)
    sy.dma_start(T.cns[:, CAPP * me:CAPP * me + CAPP], T.qos[:, 0:CAPP]).then_inc(sem.oc, 16)
    sy.wait_ge(sem.yo, 1)
    sy.dma_start(T.y[:, S:2 * S], T.yo[:]).then_inc(sem.st1, 16)
    sy.wait_ge(sem.yi, 1)
    sy.dma_start(T.y[:, S * slot_i:S * slot_i + S], T.yi[:]).then_inc(sem.st1, 16)
    sy.wait_ge(sem.yf0, 1)
    sy.dma_start(T.y[:, S * slot_o:S * slot_o + H], T.yf[:, 0:H]).then_inc(sem.st1, 16)
    sy.wait_ge(sem.st1, 48)

    v.memset(T.e1[:], 0.5).then_inc(sem.e1, 1)
    v.memset(T.ho[:], 0.0).then_inc(sem.hoz, 1)
    v.wait_ge(sem.want, 128)

    def conv(out, in_, mul, s):
        v.tensor_scalar(out, in_, mul, None, AluOpType.mult).then_inc(s, 1)

    conv(T.wo[:, 0:3], wslice(r), 4.0, sem.cvw)

    def vgather(out, off, t, s):
        v.tensor_copy(out, T.xt[:, t:4 * XC].indirect(off)).then_inc(s, 1)

    v.wait_ge(sem.lf, two * len(far))
    conv(T.fo[:], T.lf[:], 4.0, sem.cvf)
    v.wait_ge(sem.cvf, 1)
    v.wait_ge(sem.xl, 16)
    for t in (0, 1):
        vgather(T.hf[:, t:768:4], T.fo[:, 0:12], t, sem.gfv)
    v.wait_ge(sem.gfv, 2)
    v.wait_ge(sem.gfs, 2)
    v.quantize_mx(T.qf[:], T.qfs[:], T.hf[:]).then_inc(sem.qf, 1)
    v.wait_ge(sem.ln, sum(len(neng[q]) for q in near))
    conv(T.no[:, 0:9], T.ln[:, 0:9], 4.0, sem.cvn)
    v.wait_ge(sem.cvn, 1)
    for t in (0, 1):
        vgather(T.hn[:, t:576:4], T.no[:, 0:9], t, sem.gnv)
    v.wait_ge(sem.gnv, 2)
    v.wait_ge(sem.gns, 2)
    v.quantize_mx(T.qn[:], T.qns[:], T.hn[:]).then_inc(sem.qn, 1)
    v.wait_ge(sem.own, 128)
    conv(T.oo[:], T.ol[:], 4.0, sem.cvo)
    v.wait_ge(sem.slot, 128)
    conv(T.so[:], T.sl[:], 1.0, sem.cvs)
    v.wait_ge(sem.gos, 4)
    v.quantize_mx(T.qo[:], T.qos[:], T.ho[:]).then_inc(sem.qo, 1)
    v.wait_ge(sem.e2, 1)
    for b in range(4):
        v.quantize_mx(T.eq[:, 128 * b:128 * b + 128], T.es[:, 128 * b:128 * b + 128],
                      T.e2[:, 3 - b:3 - b + 512]).then_inc(sem.eq, 1)
    v.wait_ge(sem.wl, 16)
    v.quantize_mx(T.wq[:], T.ws[:], T.wt[:]).then_inc(sem.wq, 1)
    for b in (1, 3):
        v.wait_ge(sem["df%d" % b], 1)
        v.tensor_copy(window(b, far), T.pf[:, 512 * b:512 * b + 192]).then_inc(sem["wf%d" % b], 1)
    v.wait_ge(sem.cvs, 1)

    def half(b, h):
        v.tensor_tensor(T.m[:, 4 * H * h + b:4 * H * (h + 1):4],
                        T.dw[:, N * CAPP * b:N * CAPP * (b + 1)].indirect(T.so[:, 8 * h:8 * h + 8]),
                        T.xo[:, S * b + H * h:S * b + H * h + H], AluOpType.add).then_inc(sem["ga%d" % h], 1)

    for b in range(4):
        v.wait_ge(sem["xo%d" % b], 1)
        v.wait_ge(sem["wf%d" % b], 1)
        v.wait_ge(sem["wn%d" % b], 1)
        half(b, 0)
        if b == 0:
            half(b, 1)
    v.wait_ge(sem.ga0, 4)
    v.quantize_mx(T.mq[:, 0:H], T.ms[:, 0:H], T.m[:, 0:4 * H]).then_inc(sem.q0, 1)
    for b in range(1, 4):
        half(b, 1)
    v.wait_ge(sem.ga1, 4)
    v.quantize_mx(T.mq[:, H:S], T.ms[:, H:S], T.m[:, 4 * H:4 * S]).then_inc(sem.q1, 1)
    v.wait_ge(sem.pi, 1)
    v.tensor_copy(T.yi[:], T.pf[:, 512:512 + S]).then_inc(sem.yi, 1)
    v.wait_ge(sem.pf0, 1)
    v.tensor_copy(T.yf[:, 0:H], T.pf[:, 1024:1024 + H]).then_inc(sem.yf0, 1)

    def mm(out, l, ls, x, xs, s):
        pe.matmul_mx(out, l, ls, x, xs, True, True).then_inc(s, 1)

    def decode(p, c, cs, d):
        for b in range(4):
            mm(T[p][:, 512 * b:512 * b + 192], T.eq[:, 128 * b:128 * b + 128], T.es[:, 128 * b:128 * b + 128],
               T[c][:], T[cs][:], sem["%s%d" % (d, b)])

    pe.wait_ge(sem.eq, 4)
    pe.wait_ge(sem.cf, 2 * two * len(far))
    decode("pf", "cf", "cfs", "df")
    pe.wait_ge(sem.oc, 32)
    pe.wait_ge(sem.cn, 2 * sum(len(neng[q]) for q in near))
    decode("pn", "cn", "cns", "dn")
    pe.wait_ge(sem.wq, 1)
    pe.wait_ge(sem.q0, 1)
    pe.wait_ge(sem.q1, 1)
    mm(T.pf[:, 0:S], T.wq[:], T.ws[:], T.mq[:], T.ms[:], sem.po)
    pe.wait_ge(sem.mi, 3 * len(on_eng))
    mm(T.pf[:, 512:512 + S], T.wq[:], T.ws[:], T.iq[:], T.is_[:], sem.pi)
    pe.wait_ge(sem.mo, 3 * len(off_eng))
    mm(T.pf[:, 1024:1024 + H], T.wq[:], T.ws[:], T.oq[:, 0:H], T.os_[:, 0:H], sem.pf0)
    mm(T.pf[:, 1536:1536 + H], T.wq[:], T.ws[:], T.oq[:, H:S], T.os_[:, H:S], sem.pf1)
